import numpy as np
import ml_dtypes


def mxq(x, axis, fmt="e4m3"):
    dtype, down = {"e4m3": (ml_dtypes.float8_e4m3fn, 7), "e5m2": (ml_dtypes.float8_e5m2, 14)}[fmt]
    v = np.moveaxis(np.asarray(x, np.float32).astype(ml_dtypes.bfloat16).astype(np.float64), axis, -1)
    blocks = v.reshape(v.shape[:-1] + (-1, 32))
    amax = np.abs(blocks).max(-1, keepdims=True)
    byte = np.maximum(np.where(amax > 0, np.frexp(amax)[1] - 1 + 127, 0) - down, 1)
    scale = np.exp2(byte - 127.0)
    codes = (blocks / scale).astype(np.float32).astype(dtype).astype(np.float64)
    return np.moveaxis((codes * scale).reshape(v.shape), -1, axis)


WIDE = False


def mx_kscale(k):
    if not WIDE:
        return np.ones(k)
    levels = np.array([10, -10, 5, -5, 0])
    if k % 512:
        return np.exp2(np.random.permutation(np.resize(levels, k // 32))).repeat(32)
    a = np.empty((k // 512, 16))
    for p in range(k // 512):
        a[p, :8] = np.random.permutation(np.resize(levels, 8))
        for g in range(8):
            far = levels[np.abs(levels - a[p, g]) >= 10]
            a[p, g + 8] = far[np.random.randint(len(far))]
    return np.exp2(a.ravel()).repeat(32)


def f64(x):
    return np.asarray(x).astype(np.float64)


def striped(idx):
    return np.tile(idx.reshape(-1, 16).T, (8, 1)).astype(np.uint16)


def unstriped(offs):
    return offs[:16].T.reshape(-1).astype(np.int64)


K, T, S, V, N, U = 512, 1024, 512, 256, 256, 512


def setup_inputs():
    n = np.random.standard_normal
    s = mx_kscale(K)[:, None]
    return {
        "xT": (n((K, T)) * s).astype(np.float32),
        "w1": (n((K, N)) / np.sqrt(2 * K) / s).astype(np.float32),
        "w2": (n((K, N)) / np.sqrt(2 * K) / s).astype(np.float32),
        "offs": striped(np.random.permutation(T)[:S]),
        "to1": striped(np.random.permutation(U)[:V]),
        "to2": striped(np.random.permutation(U)[:V]),
    }


def reference(xT, w1, w2, offs, to1, to2):
    xq = mxq(f64(xT)[:, unstriped(offs)], 0, "e4m3")
    o0 = np.zeros((N, S))
    o0[:, unstriped(to1)] = mxq(f64(w1), 0, "e4m3").T @ xq[:, :V]
    o1 = np.zeros((N, S))
    o1[:, unstriped(to2)] = mxq(f64(w2), 0, "e4m3").T @ xq[:, V:2 * V]
    return o0 + o1

@@ -1,0 +1,146 @@
+from contextlib import ExitStack
+
+import concourse.mybir as mybir
+
+K, T, S, V, N, U = 512, 1024, 512, 256, 256, 512
+FLOPS = 2 * K * N * S
+
+F32 = mybir.dt.float32
+BF16 = mybir.dt.bfloat16
+U32 = mybir.dt.uint32
+U16 = mybir.dt.uint16
+U8 = mybir.dt.uint8
+FP8X4 = mybir.dt.float8_e4m3fn_x4
+ADD = mybir.AluOpType.add
+
+P = 128
+PACK = 4
+TAPS = 2
+BLOCKS = N // P
+LIST_COLS = V // 16
+
+
+def tile_picked_spconv_none_e_kernel(tc, xT, w1, w2, offs, to1, to2, out):
+    nc = tc.nc
+    with ExitStack() as ctx:
+        lists = ctx.enter_context(tc.tile_pool(name="lists", bufs=1))
+        keep = ctx.enter_context(tc.tile_pool(name="keep", bufs=1))
+        psum = ctx.enter_context(tc.psum_pool(name="psum", bufs=1))
+
+        offs_sb = lists.tile([P, S // 16], U16, name="offs_sb")
+        to_sb = [lists.tile([P, LIST_COLS], U16, name=f"to_sb{d}") for d in range(TAPS)]
+        planes = [keep.tile([P, T], F32, name=f"plane{j}") for j in range(PACK)]
+        w_raw = [keep.tile([P, PACK, N], F32, name=f"w_raw{d}", tag=f"w_raw{d}") for d in range(TAPS)]
+        x_rows = xT.rearrange("(p j) t -> p j t", j=PACK)
+
+        nc.sync.dma_start(out=planes[0][:], in_=x_rows[:, 0, :])
+        nc.sync.dma_start(offs_sb[:], offs)
+        nc.sync.dma_start(out=planes[1][:], in_=x_rows[:, 1, :])
+        nc.sync.dma_start(out=planes[2][:], in_=x_rows[:, 2, :])
+        nc.sync.dma_start(out=w_raw[0][:], in_=w1.rearrange("(p j) m -> p j m", j=PACK))
+        nc.sync.dma_start(out=planes[3][:], in_=x_rows[:, 3, :])
+        nc.sync.dma_start(out=w_raw[1][:], in_=w2.rearrange("(p j) m -> p j m", j=PACK))
+        nc.sync.dma_start(to_sb[0][:], to1)
+        nc.sync.dma_start(to_sb[1][:], to2)
+
+        windows = {}
+        for d in range(TAPS):
+            for b in range(BLOCKS):
+                windows[d, b] = keep.tile([P, U], F32, name=f"window{d}{b}")
+                nc.vector.memset(windows[d, b][:], 0.0)
+
+        x_bf = [keep.tile([P, V, PACK], BF16, name=f"x_bf{d}", align_bytes=64) for d in range(TAPS)]
+        x_codes = [keep.tile([P, V], U32, name=f"x_codes{d}", align_bytes=64) for d in range(TAPS)]
+        x_scales = [keep.tile([P, V], U8, name=f"x_scales{d}", align_bytes=64) for d in range(TAPS)]
+        w_bf = [keep.tile([P, N, PACK], BF16, name=f"w_bf{d}", align_bytes=64) for d in range(TAPS)]
+        w_codes = [keep.tile([P, N], U32, name=f"w_codes{d}", align_bytes=64) for d in range(TAPS)]
+        w_scales = [keep.tile([P, N], U8, name=f"w_scales{d}", align_bytes=64) for d in range(TAPS)]
+        low = keep.tile([P, 2, V], F32, name="low")
+
+        def tap_list(d):
+            return offs_sb[:, d * LIST_COLS : (d + 1) * LIST_COLS]
+
+        def gather_stepped(d, j):
+            nc.vector.tensor_copy(x_bf[d][:, :, j], planes[j][:].indirect(tap_list(d)))
+
+        def weave(d):
+            nc.scalar.copy(
+                out=x_bf[d][:, :, 0:2],
+                in_=low[:].rearrange("p j v -> p v j"),
+            )
+
+        def quantize_x(d):
+            nc.vector.quantize_mx(
+                out=x_codes[d][:].bitcast(FP8X4),
+                scales=x_scales[d][:],
+                in_=x_bf[d][:].rearrange("p v j -> p (v j)"),
+            )
+
+        def cast_w(d, cols):
+            nc.scalar.copy(
+                out=w_bf[d][:, cols, :].rearrange("p (c i) j -> p c j i", i=4),
+                in_=w_raw[d][:, :, cols].rearrange("p j (c i) -> p c j i", i=4),
+            )
+
+        def quantize_w(d, cols):
+            nc.vector.quantize_mx(
+                out=w_codes[d][:, cols].bitcast(FP8X4),
+                scales=w_scales[d][:, cols],
+                in_=w_bf[d][:, cols, :].rearrange("p m j -> p (m j)"),
+            )
+
+        def block(b):
+            return slice(b * P, (b + 1) * P)
+
+        y = {}
+
+        def product(d, b, bank, tag):
+            acc = psum.tile([P, V], F32, name=f"acc{d}{b}", tag=f"bank{bank}")
+            nc.tensor.matmul_mx(
+                out=acc[:],
+                lhsT=w_codes[d][:, block(b)].bitcast(FP8X4),
+                lhsT_scale=w_scales[d][:, block(b)],
+                rhs=x_codes[d][:].bitcast(FP8X4),
+                rhs_scale=x_scales[d][:],
+                start=True,
+                stop=True,
+            )
+            y[d, b] = keep.tile([P, V], F32, name=f"y{d}{b}", tag=tag)
+            nc.scalar.copy(out=y[d, b][:], in_=acc[:])
+
+        def scatter(d, b):
+            nc.vector.tensor_copy(windows[d, b][:].indirect(to_sb[d][:]), y[d, b][:])
+
+        def finish(b, engine, pieces):
+            total = keep.tile([P, U], F32, name=f"total{b}")
+            for h in range(pieces):
+                cols = slice(h * U // pieces, (h + 1) * U // pieces)
+                engine.tensor_tensor(total[:, cols], windows[0, b][:, cols], windows[1, b][:, cols], ADD)
+                nc.sync.dma_start(out=out[block(b), cols], in_=total[:, cols])
+
+        for j in range(2):
+            nc.vector.tensor_copy(low[:, j, :], planes[j][:].indirect(tap_list(1)))
+            gather_stepped(0, j)
+        weave(1)
+        gather_stepped(0, 2)
+        gather_stepped(1, 2)
+        cast_w(0, block(0))
+        cast_w(0, block(1))
+        quantize_w(0, block(0))
+        gather_stepped(0, 3)
+        quantize_w(0, block(1))
+        quantize_x(0)
+        gather_stepped(1, 3)
+        cast_w(1, slice(0, N))
+        quantize_x(1)
+        quantize_w(1, slice(0, N))
+        product(0, 0, 0, "w_raw1")
+        product(1, 0, 1, "y10")
+        scatter(0, 0)
+        product(0, 1, 1, "y01")
+        product(1, 1, 0, "y11")
+        scatter(1, 0)
+        finish(0, nc.vector, 1)
+        scatter(0, 1)
+        scatter(1, 1)
+        finish(1, nc.vector, 2)

@@ -140,7 +140,7 @@ def tile_picked_spconv_none_e_kernel(tc, xT, w1, w2, offs, to1, to2, out):
         product(0, 1, 1, "y01")
         product(1, 1, 0, "y11")
         scatter(1, 0)
-        finish(0, nc.vector, 1)
+        finish(0, nc.gpsimd, 1)
         scatter(0, 1)
         scatter(1, 1)
         finish(1, nc.vector, 2)

@@ -7,6 +7,7 @@ FLOPS = 2 * K * N * S
 
 F32 = mybir.dt.float32
 BF16 = mybir.dt.bfloat16
+I32 = mybir.dt.int32
 U32 = mybir.dt.uint32
 U16 = mybir.dt.uint16
 U8 = mybir.dt.uint8
@@ -30,17 +31,16 @@ def tile_picked_spconv_none_e_kernel(tc, xT, w1, w2, offs, to1, to2, out):
         offs_sb = lists.tile([P, S // 16], U16, name="offs_sb")
         to_sb = [lists.tile([P, LIST_COLS], U16, name=f"to_sb{d}") for d in range(TAPS)]
         planes = [keep.tile([P, T], F32, name=f"plane{j}") for j in range(PACK)]
-        w_raw = [keep.tile([P, PACK, N], F32, name=f"w_raw{d}", tag=f"w_raw{d}") for d in range(TAPS)]
+        w_raw = [keep.tile([P, PACK, N], F32, name=f"w_raw{d}", tag=f"w_raw{d}", align_bytes=64) for d in range(TAPS)]
         x_rows = xT.rearrange("(p j) t -> p j t", j=PACK)
 
         nc.sync.dma_start(out=planes[0][:], in_=x_rows[:, 0, :])
         nc.sync.dma_start(offs_sb[:], offs)
-        nc.sync.dma_start(out=planes[1][:], in_=x_rows[:, 1, :])
-        nc.sync.dma_start(out=planes[2][:], in_=x_rows[:, 2, :])
+        for j in range(1, PACK):
+            nc.sync.dma_start(out=planes[j][:], in_=x_rows[:, j, :])
         nc.sync.dma_start(out=w_raw[0][:], in_=w1.rearrange("(p j) m -> p j m", j=PACK))
-        nc.sync.dma_start(out=planes[3][:], in_=x_rows[:, 3, :])
-        nc.sync.dma_start(out=w_raw[1][:], in_=w2.rearrange("(p j) m -> p j m", j=PACK))
         nc.sync.dma_start(to_sb[0][:], to1)
+        nc.sync.dma_start(out=w_raw[1][:], in_=w2.rearrange("(p j) m -> p j m", j=PACK))
         nc.sync.dma_start(to_sb[1][:], to2)
 
         windows = {}
@@ -49,25 +49,14 @@ def tile_picked_spconv_none_e_kernel(tc, xT, w1, w2, offs, to1, to2, out):
                 windows[d, b] = keep.tile([P, U], F32, name=f"window{d}{b}")
                 nc.vector.memset(windows[d, b][:], 0.0)
 
-        x_bf = [keep.tile([P, V, PACK], BF16, name=f"x_bf{d}", align_bytes=64) for d in range(TAPS)]
+        x_bf = {0: keep.tile([P, V, PACK], BF16, name="x_bf0", align_bytes=64)}
         x_codes = [keep.tile([P, V], U32, name=f"x_codes{d}", align_bytes=64) for d in range(TAPS)]
         x_scales = [keep.tile([P, V], U8, name=f"x_scales{d}", align_bytes=64) for d in range(TAPS)]
-        w_bf = [keep.tile([P, N, PACK], BF16, name=f"w_bf{d}", align_bytes=64) for d in range(TAPS)]
-        w_codes = [keep.tile([P, N], U32, name=f"w_codes{d}", align_bytes=64) for d in range(TAPS)]
-        w_scales = [keep.tile([P, N], U8, name=f"w_scales{d}", align_bytes=64) for d in range(TAPS)]
-        low = keep.tile([P, 2, V], F32, name="low")
+        picked = keep.tile([P, 2, S], F32, name="picked")
+        pairs = keep.tile([P, 2, V, 2], BF16, name="pairs", align_bytes=64)
 
         def tap_list(d):
             return offs_sb[:, d * LIST_COLS : (d + 1) * LIST_COLS]
-
-        def gather_stepped(d, j):
-            nc.vector.tensor_copy(x_bf[d][:, :, j], planes[j][:].indirect(tap_list(d)))
-
-        def weave(d):
-            nc.scalar.copy(
-                out=x_bf[d][:, :, 0:2],
-                in_=low[:].rearrange("p j v -> p v j"),
-            )
 
         def quantize_x(d):
             nc.vector.quantize_mx(
@@ -76,36 +65,43 @@ def tile_picked_spconv_none_e_kernel(tc, xT, w1, w2, offs, to1, to2, out):
                 in_=x_bf[d][:].rearrange("p v j -> p (v j)"),
             )
 
-        def cast_w(d, cols):
-            nc.scalar.copy(
-                out=w_bf[d][:, cols, :].rearrange("p (c i) j -> p c j i", i=4),
-                in_=w_raw[d][:, :, cols].rearrange("p j (c i) -> p c j i", i=4),
-            )
-
-        def quantize_w(d, cols):
-            nc.vector.quantize_mx(
-                out=w_codes[d][:, cols].bitcast(FP8X4),
-                scales=w_scales[d][:, cols],
-                in_=w_bf[d][:, cols, :].rearrange("p m j -> p (m j)"),
-            )
-
         def block(b):
             return slice(b * P, (b + 1) * P)
 
+        w_codes, w_scales = {}, {}
+
+        def prepare_w(copy, d, cols, label, bf_tag, codes_tag, scales_tag):
+            width = cols.stop - cols.start
+            w_bf = keep.tile([P, width, PACK], BF16, name=f"w_bf{label}", tag=bf_tag, align_bytes=64)
+            codes = keep.tile([P, width], U32, name=f"w_codes{label}", tag=codes_tag, align_bytes=64)
+            scales = keep.tile([P, width], U8, name=f"w_scales{label}", tag=scales_tag, align_bytes=64)
+            copy(
+                out=w_bf[:].rearrange("p (c i) j -> p c j i", i=4),
+                in_=w_raw[d][:, :, cols].rearrange("p j (c i) -> p c j i", i=4),
+            )
+            nc.vector.quantize_mx(
+                out=codes[:].bitcast(FP8X4),
+                scales=scales[:],
+                in_=w_bf[:].rearrange("p m j -> p (m j)"),
+            )
+            for b in range(width // P):
+                w_codes[d, cols.start // P + b] = codes[:, block(b)]
+                w_scales[d, cols.start // P + b] = scales[:, block(b)]
+
         y = {}
 
-        def product(d, b, bank, tag):
-            acc = psum.tile([P, V], F32, name=f"acc{d}{b}", tag=f"bank{bank}")
+        def product(d, b, tag):
+            acc = psum.tile([P, V], F32, name=f"acc{d}{b}")
             nc.tensor.matmul_mx(
                 out=acc[:],
-                lhsT=w_codes[d][:, block(b)].bitcast(FP8X4),
-                lhsT_scale=w_scales[d][:, block(b)],
+                lhsT=w_codes[d, b].bitcast(FP8X4),
+                lhsT_scale=w_scales[d, b],
                 rhs=x_codes[d][:].bitcast(FP8X4),
                 rhs_scale=x_scales[d][:],
                 start=True,
                 stop=True,
             )
-            y[d, b] = keep.tile([P, V], F32, name=f"y{d}{b}", tag=tag)
+            y[d, b] = keep.tile([P, V], F32, name=f"y{d}{b}", tag=tag, align_bytes=64)
             nc.scalar.copy(out=y[d, b][:], in_=acc[:])
 
         def scatter(d, b):
@@ -119,28 +115,29 @@ def tile_picked_spconv_none_e_kernel(tc, xT, w1, w2, offs, to1, to2, out):
                 nc.sync.dma_start(out=out[block(b), cols], in_=total[:, cols])
 
         for j in range(2):
-            nc.vector.tensor_copy(low[:, j, :], planes[j][:].indirect(tap_list(1)))
-            gather_stepped(0, j)
-        weave(1)
-        gather_stepped(0, 2)
-        gather_stepped(1, 2)
-        cast_w(0, block(0))
-        cast_w(0, block(1))
-        quantize_w(0, block(0))
-        gather_stepped(0, 3)
-        quantize_w(0, block(1))
+            nc.vector.tensor_copy(picked[:, j, :], planes[j][:].indirect(offs_sb[:]))
+        nc.scalar.copy(out=x_bf[0][:, :, 0:2], in_=picked[:, :, 0:V].rearrange("p j v -> p v j"))
+        nc.scalar.copy(out=pairs[:, 0, :, :], in_=picked[:, :, V:S].rearrange("p j v -> p v j"))
+        for j in range(2, PACK):
+            nc.vector.tensor_copy(x_bf[0][:, :, j], planes[j][:].indirect(tap_list(0)))
+            nc.vector.tensor_copy(pairs[:, 1, :, j - 2], planes[j][:].indirect(tap_list(1)))
         quantize_x(0)
-        gather_stepped(1, 3)
-        cast_w(1, slice(0, N))
+        prepare_w(nc.scalar.copy, 0, block(0), "00", "first_bf", "first_codes", "w_scales00")
+        x_bf[1] = keep.tile([P, V, PACK], BF16, name="x_bf1", tag="first_bf", align_bytes=64)
+        nc.vector.tensor_copy(
+            out=x_bf[1][:].rearrange("p v j -> p (v j)").bitcast(I32).rearrange("p (v h) -> p v h", h=2),
+            in_=pairs[:].rearrange("p h v e -> p (h v e)").bitcast(I32).rearrange("p (h v) -> p v h", h=2),
+        )
+        prepare_w(nc.scalar.copy, 0, block(1), "01", "w_bf01", "w_codes01", "w_scales01")
         quantize_x(1)
-        quantize_w(1, slice(0, N))
-        product(0, 0, 0, "w_raw1")
-        product(1, 0, 1, "y10")
+        product(0, 0, "y00")
         scatter(0, 0)
-        product(0, 1, 1, "y01")
-        product(1, 1, 0, "y11")
+        prepare_w(nc.scalar.copy, 1, slice(0, N), "1", "first_codes", "w_codes1", "w_scales1")
+        product(0, 1, "w_raw1")
+        scatter(0, 1)
+        product(1, 0, "y10")
         scatter(1, 0)
         finish(0, nc.gpsimd, 1)
-        scatter(0, 1)
+        product(1, 1, "y11")
         scatter(1, 1)
         finish(1, nc.vector, 2)

@@ -13,6 +13,7 @@ U16 = mybir.dt.uint16
 U8 = mybir.dt.uint8
 FP8X4 = mybir.dt.float8_e4m3fn_x4
 ADD = mybir.AluOpType.add
+COPY = mybir.ActivationFunctionType.Copy
 
 P = 128
 PACK = 4
@@ -36,7 +37,7 @@ def tile_picked_spconv_none_e_kernel(tc, xT, w1, w2, offs, to1, to2, out):
 
         nc.sync.dma_start(out=planes[0][:], in_=x_rows[:, 0, :])
         nc.sync.dma_start(offs_sb[:], offs)
-        for j in range(1, PACK):
+        for j in (2, 3, 1):
             nc.sync.dma_start(out=planes[j][:], in_=x_rows[:, j, :])
         nc.sync.dma_start(out=w_raw[0][:], in_=w1.rearrange("(p j) m -> p j m", j=PACK))
         nc.sync.dma_start(to_sb[0][:], to1)
@@ -52,7 +53,8 @@ def tile_picked_spconv_none_e_kernel(tc, xT, w1, w2, offs, to1, to2, out):
         x_bf = {0: keep.tile([P, V, PACK], BF16, name="x_bf0", align_bytes=64)}
         x_codes = [keep.tile([P, V], U32, name=f"x_codes{d}", align_bytes=64) for d in range(TAPS)]
         x_scales = [keep.tile([P, V], U8, name=f"x_scales{d}", align_bytes=64) for d in range(TAPS)]
-        picked = keep.tile([P, 2, S], F32, name="picked")
+        picked = keep.tile([P, 2, V], F32, name="picked")
+        rounded = [keep.tile([P, T], BF16, name=f"rounded{e}") for e in range(2)]
         pairs = keep.tile([P, 2, V, 2], BF16, name="pairs", align_bytes=64)
 
         def tap_list(d):
@@ -75,10 +77,11 @@ def tile_picked_spconv_none_e_kernel(tc, xT, w1, w2, offs, to1, to2, out):
             w_bf = keep.tile([P, width, PACK], BF16, name=f"w_bf{label}", tag=bf_tag, align_bytes=64)
             codes = keep.tile([P, width], U32, name=f"w_codes{label}", tag=codes_tag, align_bytes=64)
             scales = keep.tile([P, width], U8, name=f"w_scales{label}", tag=scales_tag, align_bytes=64)
-            copy(
-                out=w_bf[:].rearrange("p (c i) j -> p c j i", i=4),
-                in_=w_raw[d][:, :, cols].rearrange("p j (c i) -> p c j i", i=4),
-            )
+            if d == 0:
+                source = w_raw[d][:, :, cols].rearrange("p (a b) (c i) -> p c a b i", b=2, i=4)
+            else:
+                source = w_raw[d][:, :, cols].rearrange("p (a b) (c i) -> p c b a i", b=2, i=4)
+            copy(out=w_bf[:].rearrange("p (c i) (h e) -> p c h e i", e=2, i=4), in_=source)
             nc.vector.quantize_mx(
                 out=codes[:].bitcast(FP8X4),
                 scales=scales[:],
@@ -114,13 +117,16 @@ def tile_picked_spconv_none_e_kernel(tc, xT, w1, w2, offs, to1, to2, out):
                 engine.tensor_tensor(total[:, cols], windows[0, b][:, cols], windows[1, b][:, cols], ADD)
                 nc.sync.dma_start(out=out[block(b), cols], in_=total[:, cols])
 
-        for j in range(2):
-            nc.vector.tensor_copy(picked[:, j, :], planes[j][:].indirect(offs_sb[:]))
-        nc.scalar.copy(out=x_bf[0][:, :, 0:2], in_=picked[:, :, 0:V].rearrange("p j v -> p v j"))
-        nc.scalar.copy(out=pairs[:, 0, :, :], in_=picked[:, :, V:S].rearrange("p j v -> p v j"))
-        for j in range(2, PACK):
-            nc.vector.tensor_copy(x_bf[0][:, :, j], planes[j][:].indirect(tap_list(0)))
-            nc.vector.tensor_copy(pairs[:, 1, :, j - 2], planes[j][:].indirect(tap_list(1)))
+        for e in range(2):
+            nc.scalar.activation(rounded[e][:], planes[2 * e][:], COPY)
+            nc.scalar.activation(pairs[:, 0, :, e], rounded[e][:].indirect(tap_list(1)), COPY)
+        nc.vector.tensor_copy(x_bf[0][:, :, 0], planes[0][:].indirect(tap_list(0)))
+        for e in range(2):
+            nc.vector.tensor_copy(picked[:, e, :], planes[2 + e][:].indirect(tap_list(0)))
+        nc.scalar.copy(out=x_bf[0][:, :, 2:4], in_=picked[:].rearrange("p j v -> p v j"))
+        nc.vector.tensor_copy(pairs[:, 1, :, 1], planes[3][:].indirect(tap_list(1)))
+        nc.vector.tensor_copy(x_bf[0][:, :, 1], planes[1][:].indirect(tap_list(0)))
+        nc.vector.tensor_copy(pairs[:, 1, :, 0], planes[1][:].indirect(tap_list(1)))
         quantize_x(0)
         prepare_w(nc.scalar.copy, 0, block(0), "00", "first_bf", "first_codes", "w_scales00")
         x_bf[1] = keep.tile([P, V, PACK], BF16, name="x_bf1", tag="first_bf", align_bytes=64)

@@ -32,14 +32,17 @@ def tile_picked_spconv_none_e_kernel(tc, xT, w1, w2, offs, to1, to2, out):
         offs_sb = lists.tile([P, S // 16], U16, name="offs_sb")
         to_sb = [lists.tile([P, LIST_COLS], U16, name=f"to_sb{d}") for d in range(TAPS)]
         planes = [keep.tile([P, T], F32, name=f"plane{j}") for j in range(PACK)]
-        w_raw = [keep.tile([P, PACK, N], F32, name=f"w_raw{d}", tag=f"w_raw{d}", align_bytes=64) for d in range(TAPS)]
+        w_raw = {1: keep.tile([P, PACK, N], F32, name="w_raw1", tag="w_raw1", align_bytes=64)}
         x_rows = xT.rearrange("(p j) t -> p j t", j=PACK)
 
         nc.sync.dma_start(out=planes[0][:], in_=x_rows[:, 0, :])
         nc.sync.dma_start(offs_sb[:], offs)
         for j in (2, 3, 1):
             nc.sync.dma_start(out=planes[j][:], in_=x_rows[:, j, :])
-        nc.sync.dma_start(out=w_raw[0][:], in_=w1.rearrange("(p j) m -> p j m", j=PACK))
+        w1_rows = w1.rearrange("(p j) m -> p j m", j=PACK)
+        w1_raw = [keep.tile([P, PACK, P], F32, name=f"w1_raw{b}", tag=f"w1_raw{b}", align_bytes=64) for b in range(BLOCKS)]
+        for b in range(BLOCKS):
+            nc.sync.dma_start(out=w1_raw[b][:], in_=w1_rows[:, :, b * P : (b + 1) * P])
         nc.sync.dma_start(to_sb[0][:], to1)
         nc.sync.dma_start(out=w_raw[1][:], in_=w2.rearrange("(p j) m -> p j m", j=PACK))
         nc.sync.dma_start(to_sb[1][:], to2)
@@ -78,7 +81,7 @@ def tile_picked_spconv_none_e_kernel(tc, xT, w1, w2, offs, to1, to2, out):
             codes = keep.tile([P, width], U32, name=f"w_codes{label}", tag=codes_tag, align_bytes=64)
             scales = keep.tile([P, width], U8, name=f"w_scales{label}", tag=scales_tag, align_bytes=64)
             if d == 0:
-                source = w_raw[d][:, :, cols].rearrange("p (a b) (c i) -> p c a b i", b=2, i=4)
+                source = w1_raw[cols.start // P][:].rearrange("p (a b) (c i) -> p c a b i", b=2, i=4)
             else:
                 source = w_raw[d][:, :, cols].rearrange("p (a b) (c i) -> p c b a i", b=2, i=4)
             copy(out=w_bf[:].rearrange("p (c i) (h e) -> p c h e i", e=2, i=4), in_=source)
@@ -117,10 +120,12 @@ def tile_picked_spconv_none_e_kernel(tc, xT, w1, w2, offs, to1, to2, out):
                 engine.tensor_tensor(total[:, cols], windows[0, b][:, cols], windows[1, b][:, cols], ADD)
                 nc.sync.dma_start(out=out[block(b), cols], in_=total[:, cols])
 
-        for e in range(2):
-            nc.scalar.activation(rounded[e][:], planes[2 * e][:], COPY)
-            nc.scalar.activation(pairs[:, 0, :, e], rounded[e][:].indirect(tap_list(1)), COPY)
+        nc.scalar.activation(rounded[0][:], planes[0][:], COPY)
+        nc.scalar.activation(pairs[:, 0, :, 0], rounded[0][:].indirect(tap_list(1)), COPY)
         nc.vector.tensor_copy(x_bf[0][:, :, 0], planes[0][:].indirect(tap_list(0)))
+        nc.vector.tensor_copy(rounded[1][:, : T // 2], planes[2][:, : T // 2])
+        nc.scalar.activation(rounded[1][:, T // 2 :], planes[2][:, T // 2 :], COPY)
+        nc.scalar.activation(pairs[:, 0, :, 1], rounded[1][:].indirect(tap_list(1)), COPY)
         for e in range(2):
             nc.vector.tensor_copy(picked[:, e, :], planes[2 + e][:].indirect(tap_list(0)))
         nc.scalar.copy(out=x_bf[0][:, :, 2:4], in_=picked[:].rearrange("p j v -> p v j"))
@@ -129,14 +134,27 @@ def tile_picked_spconv_none_e_kernel(tc, xT, w1, w2, offs, to1, to2, out):
         nc.vector.tensor_copy(pairs[:, 1, :, 0], planes[1][:].indirect(tap_list(1)))
         quantize_x(0)
         prepare_w(nc.scalar.copy, 0, block(0), "00", "first_bf", "first_codes", "w_scales00")
-        x_bf[1] = keep.tile([P, V, PACK], BF16, name="x_bf1", tag="first_bf", align_bytes=64)
+        x_bf[1] = keep.tile([P, V, PACK], BF16, name="x_bf1", tag="w1_raw0", align_bytes=64)
         nc.vector.tensor_copy(
             out=x_bf[1][:].rearrange("p v j -> p (v j)").bitcast(I32).rearrange("p (v h) -> p v h", h=2),
             in_=pairs[:].rearrange("p h v e -> p (h v e)").bitcast(I32).rearrange("p (h v) -> p v h", h=2),
         )
         prepare_w(nc.scalar.copy, 0, block(1), "01", "w_bf01", "w_codes01", "w_scales01")
         quantize_x(1)
-        product(0, 0, "y00")
+        y[0, 0] = keep.tile([P, V], F32, name="y00")
+        for h in range(2):
+            cols = slice(h * P, (h + 1) * P)
+            acc = psum.tile([P, P], F32, name=f"acc_first{h}")
+            nc.tensor.matmul_mx(
+                out=acc[:],
+                lhsT=w_codes[0, 0].bitcast(FP8X4),
+                lhsT_scale=w_scales[0, 0],
+                rhs=x_codes[0][:, cols].bitcast(FP8X4),
+                rhs_scale=x_scales[0][:, cols],
+                start=True,
+                stop=True,
+            )
+            nc.scalar.copy(out=y[0, 0][:, cols], in_=acc[:])
         scatter(0, 0)
         prepare_w(nc.scalar.copy, 1, slice(0, N), "1", "first_codes", "w_codes1", "w_scales1")
         product(0, 1, "w_raw1")

@@ -113,10 +113,10 @@ def tile_picked_spconv_none_e_kernel(tc, xT, w1, w2, offs, to1, to2, out):
         def scatter(d, b):
             nc.vector.tensor_copy(windows[d, b][:].indirect(to_sb[d][:]), y[d, b][:])
 
-        def finish(b, engine, pieces):
+        def finish(b, engine, edges):
             total = keep.tile([P, U], F32, name=f"total{b}")
-            for h in range(pieces):
-                cols = slice(h * U // pieces, (h + 1) * U // pieces)
+            for h in range(len(edges) - 1):
+                cols = slice(edges[h], edges[h + 1])
                 engine.tensor_tensor(total[:, cols], windows[0, b][:, cols], windows[1, b][:, cols], ADD)
                 nc.sync.dma_start(out=out[block(b), cols], in_=total[:, cols])
 
@@ -161,7 +161,7 @@ def tile_picked_spconv_none_e_kernel(tc, xT, w1, w2, offs, to1, to2, out):
         scatter(0, 1)
         product(1, 0, "y10")
         scatter(1, 0)
-        finish(0, nc.gpsimd, 1)
+        finish(0, nc.gpsimd, (0, U // 2, U))
         product(1, 1, "y11")
         scatter(1, 1)
-        finish(1, nc.vector, 2)
+        finish(1, nc.vector, (0, 192, 384, U))

@@ -113,12 +113,12 @@ def tile_picked_spconv_none_e_kernel(tc, xT, w1, w2, offs, to1, to2, out):
         def scatter(d, b):
             nc.vector.tensor_copy(windows[d, b][:].indirect(to_sb[d][:]), y[d, b][:])
 
-        def finish(b, engine, edges):
+        def finish(b, engine, queue, edges):
             total = keep.tile([P, U], F32, name=f"total{b}")
             for h in range(len(edges) - 1):
                 cols = slice(edges[h], edges[h + 1])
                 engine.tensor_tensor(total[:, cols], windows[0, b][:, cols], windows[1, b][:, cols], ADD)
-                nc.sync.dma_start(out=out[block(b), cols], in_=total[:, cols])
+                queue.dma_start(out=out[block(b), cols], in_=total[:, cols])
 
         nc.scalar.activation(rounded[0][:], planes[0][:], COPY)
         nc.scalar.activation(pairs[:, 0, :, 0], rounded[0][:].indirect(tap_list(1)), COPY)
@@ -161,7 +161,7 @@ def tile_picked_spconv_none_e_kernel(tc, xT, w1, w2, offs, to1, to2, out):
         scatter(0, 1)
         product(1, 0, "y10")
         scatter(1, 0)
-        finish(0, nc.gpsimd, (0, U // 2, U))
+        finish(0, nc.gpsimd, nc.scalar, (0, 320, U))
         product(1, 1, "y11")
         scatter(1, 1)
-        finish(1, nc.vector, (0, 192, 384, U))
+        finish(1, nc.vector, nc.sync, (0, 192, 384, U))

@@ -20,6 +20,7 @@ PACK = 4
 TAPS = 2
 BLOCKS = N // P
 LIST_COLS = V // 16
+RAW_BYTES = PACK * P * 4
 
 
 def tile_picked_spconv_none_e_kernel(tc, xT, w1, w2, offs, to1, to2, out):
@@ -27,91 +28,88 @@ def tile_picked_spconv_none_e_kernel(tc, xT, w1, w2, offs, to1, to2, out):
     with ExitStack() as ctx:
         lists = ctx.enter_context(tc.tile_pool(name="lists", bufs=1))
         keep = ctx.enter_context(tc.tile_pool(name="keep", bufs=1))
+        reused = ctx.enter_context(tc.tile_pool(name="reused", bufs=1))
         psum = ctx.enter_context(tc.psum_pool(name="psum", bufs=1))
 
         offs_sb = lists.tile([P, S // 16], U16, name="offs_sb")
         to_sb = [lists.tile([P, LIST_COLS], U16, name=f"to_sb{d}") for d in range(TAPS)]
         planes = [keep.tile([P, T], F32, name=f"plane{j}") for j in range(PACK)]
-        w_raw = {1: keep.tile([P, PACK, N], F32, name="w_raw1", tag="w_raw1", align_bytes=64)}
         x_rows = xT.rearrange("(p j) t -> p j t", j=PACK)
+        w_raw = {(d, 0): keep.tile([P, PACK, P], F32, name=f"w_raw{d}0") for d in range(TAPS)}
+        for d in range(TAPS):
+            w_raw[d, 1] = reused.tile([P, PACK, P], F32, name=f"w_raw{d}1", offset=d * RAW_BYTES)
+        w_rows = [w.rearrange("(p j) m -> p j m", j=PACK) for w in (w1, w2)]
 
         nc.sync.dma_start(out=planes[0][:], in_=x_rows[:, 0, :])
         nc.sync.dma_start(offs_sb[:], offs)
-        for j in (2, 3, 1):
+        for j in range(1, PACK):
             nc.sync.dma_start(out=planes[j][:], in_=x_rows[:, j, :])
-        w1_rows = w1.rearrange("(p j) m -> p j m", j=PACK)
-        w1_raw = [keep.tile([P, PACK, P], F32, name=f"w1_raw{b}", tag=f"w1_raw{b}", align_bytes=64) for b in range(BLOCKS)]
-        for b in range(BLOCKS):
-            nc.sync.dma_start(out=w1_raw[b][:], in_=w1_rows[:, :, b * P : (b + 1) * P])
+        for d in range(TAPS):
+            nc.sync.dma_start(out=w_raw[d, 0][:], in_=w_rows[d][:, :, 0:P])
         nc.sync.dma_start(to_sb[0][:], to1)
-        nc.sync.dma_start(out=w_raw[1][:], in_=w2.rearrange("(p j) m -> p j m", j=PACK))
         nc.sync.dma_start(to_sb[1][:], to2)
+        for d in range(TAPS):
+            nc.sync.dma_start(out=w_raw[d, 1][:], in_=w_rows[d][:, :, P:N])
 
         windows = {}
         for d in range(TAPS):
             for b in range(BLOCKS):
                 windows[d, b] = keep.tile([P, U], F32, name=f"window{d}{b}")
-                nc.vector.memset(windows[d, b][:], 0.0)
+                if d == 0:
+                    nc.vector.memset(windows[d, b][:], 0.0)
+                else:
+                    nc.scalar.activation(windows[d, b][:], windows[0, b][:], COPY)
 
-        x_bf = {0: keep.tile([P, V, PACK], BF16, name="x_bf0", align_bytes=64)}
+        x_bf = [keep.tile([P, V, PACK], BF16, name=f"x_bf{d}", align_bytes=64) for d in range(TAPS)]
         x_codes = [keep.tile([P, V], U32, name=f"x_codes{d}", align_bytes=64) for d in range(TAPS)]
         x_scales = [keep.tile([P, V], U8, name=f"x_scales{d}", align_bytes=64) for d in range(TAPS)]
-        picked = keep.tile([P, 2, V], F32, name="picked")
-        rounded = [keep.tile([P, T], BF16, name=f"rounded{e}") for e in range(2)]
-        pairs = keep.tile([P, 2, V, 2], BF16, name="pairs", align_bytes=64)
+        picked = keep.tile([P, PACK, V], BF16, name="picked")
 
         def tap_list(d):
             return offs_sb[:, d * LIST_COLS : (d + 1) * LIST_COLS]
 
-        def quantize_x(d):
-            nc.vector.quantize_mx(
-                out=x_codes[d][:].bitcast(FP8X4),
-                scales=x_scales[d][:],
-                in_=x_bf[d][:].rearrange("p v j -> p (v j)"),
-            )
-
         def block(b):
             return slice(b * P, (b + 1) * P)
 
-        w_codes, w_scales = {}, {}
+        def quantize(codes, scales, src):
+            nc.vector.quantize_mx(out=codes[:].bitcast(FP8X4), scales=scales[:], in_=src[:].rearrange("p v j -> p (v j)"))
 
-        def prepare_w(copy, d, cols, label, bf_tag, codes_tag, scales_tag):
-            width = cols.stop - cols.start
-            w_bf = keep.tile([P, width, PACK], BF16, name=f"w_bf{label}", tag=bf_tag, align_bytes=64)
-            codes = keep.tile([P, width], U32, name=f"w_codes{label}", tag=codes_tag, align_bytes=64)
-            scales = keep.tile([P, width], U8, name=f"w_scales{label}", tag=scales_tag, align_bytes=64)
-            if d == 0:
-                source = w1_raw[cols.start // P][:].rearrange("p (a b) (c i) -> p c a b i", b=2, i=4)
-            else:
-                source = w_raw[d][:, :, cols].rearrange("p (a b) (c i) -> p c b a i", b=2, i=4)
-            copy(out=w_bf[:].rearrange("p (c i) (h e) -> p c h e i", e=2, i=4), in_=source)
-            nc.vector.quantize_mx(
-                out=codes[:].bitcast(FP8X4),
-                scales=scales[:],
-                in_=w_bf[:].rearrange("p m j -> p (m j)"),
+        w_bf, w_codes, w_scales = {}, {}, {}
+
+        def cast_w(copy, d, b):
+            w_bf[d, b] = keep.tile([P, P, PACK], BF16, name=f"w_bf{d}{b}", align_bytes=64)
+            copy(
+                out=w_bf[d, b][:].rearrange("p (c i) j -> p c j i", i=4),
+                in_=w_raw[d, b][:].rearrange("p j (c i) -> p c j i", i=4),
             )
-            for b in range(width // P):
-                w_codes[d, cols.start // P + b] = codes[:, block(b)]
-                w_scales[d, cols.start // P + b] = scales[:, block(b)]
 
-        y = {}
+        def quantize_w(d, b):
+            w_codes[d, b] = keep.tile([P, P], U32, name=f"w_codes{d}{b}", align_bytes=64)
+            w_scales[d, b] = keep.tile([P, P], U8, name=f"w_scales{d}{b}", align_bytes=64)
+            quantize(w_codes[d, b], w_scales[d, b], w_bf[d, b])
 
-        def product(d, b, tag):
-            acc = psum.tile([P, V], F32, name=f"acc{d}{b}")
+        acc, y = {}, {}
+
+        def product(d, b):
+            acc[d, b] = psum.tile([P, V], F32, name=f"acc{d}{b}")
             nc.tensor.matmul_mx(
-                out=acc[:],
-                lhsT=w_codes[d, b].bitcast(FP8X4),
-                lhsT_scale=w_scales[d, b],
+                out=acc[d, b][:],
+                lhsT=w_codes[d, b][:].bitcast(FP8X4),
+                lhsT_scale=w_scales[d, b][:],
                 rhs=x_codes[d][:].bitcast(FP8X4),
                 rhs_scale=x_scales[d][:],
                 start=True,
                 stop=True,
             )
-            y[d, b] = keep.tile([P, V], F32, name=f"y{d}{b}", tag=tag, align_bytes=64)
-            nc.scalar.copy(out=y[d, b][:], in_=acc[:])
 
-        def scatter(d, b):
-            nc.vector.tensor_copy(windows[d, b][:].indirect(to_sb[d][:]), y[d, b][:])
+        def empty(copy, d, b):
+            copy(out=y[b][:, d, :], in_=acc[d, b][:])
+
+        def scatter_v(d, b):
+            nc.vector.tensor_copy(windows[d, b][:].indirect(to_sb[d][:]), y[b][:, d, :])
+
+        def scatter_s(d, b):
+            nc.scalar.activation(windows[d, b][:].indirect(to_sb[d][:]), y[b][:, d, :], COPY)
 
         def finish(b, engine, queue, edges):
             total = keep.tile([P, U], F32, name=f"total{b}")
@@ -120,48 +118,36 @@ def tile_picked_spconv_none_e_kernel(tc, xT, w1, w2, offs, to1, to2, out):
                 engine.tensor_tensor(total[:, cols], windows[0, b][:, cols], windows[1, b][:, cols], ADD)
                 queue.dma_start(out=out[block(b), cols], in_=total[:, cols])
 
-        nc.scalar.activation(rounded[0][:], planes[0][:], COPY)
-        nc.scalar.activation(pairs[:, 0, :, 0], rounded[0][:].indirect(tap_list(1)), COPY)
-        nc.vector.tensor_copy(x_bf[0][:, :, 0], planes[0][:].indirect(tap_list(0)))
-        nc.vector.tensor_copy(rounded[1][:, : T // 2], planes[2][:, : T // 2])
-        nc.scalar.activation(rounded[1][:, T // 2 :], planes[2][:, T // 2 :], COPY)
-        nc.scalar.activation(pairs[:, 0, :, 1], rounded[1][:].indirect(tap_list(1)), COPY)
-        for e in range(2):
-            nc.vector.tensor_copy(picked[:, e, :], planes[2 + e][:].indirect(tap_list(0)))
-        nc.scalar.copy(out=x_bf[0][:, :, 2:4], in_=picked[:].rearrange("p j v -> p v j"))
-        nc.vector.tensor_copy(pairs[:, 1, :, 1], planes[3][:].indirect(tap_list(1)))
-        nc.vector.tensor_copy(x_bf[0][:, :, 1], planes[1][:].indirect(tap_list(0)))
-        nc.vector.tensor_copy(pairs[:, 1, :, 0], planes[1][:].indirect(tap_list(1)))
-        quantize_x(0)
-        prepare_w(nc.scalar.copy, 0, block(0), "00", "first_bf", "first_codes", "w_scales00")
-        x_bf[1] = keep.tile([P, V, PACK], BF16, name="x_bf1", tag="w1_raw0", align_bytes=64)
-        nc.vector.tensor_copy(
-            out=x_bf[1][:].rearrange("p v j -> p (v j)").bitcast(I32).rearrange("p (v h) -> p v h", h=2),
-            in_=pairs[:].rearrange("p h v e -> p (h v e)").bitcast(I32).rearrange("p (h v) -> p v h", h=2),
+        for j in range(PACK):
+            nc.vector.tensor_copy(x_bf[0][:, :, j], planes[j][:].indirect(tap_list(0)))
+            nc.scalar.activation(picked[:, j, :], planes[j][:].indirect(tap_list(1)), COPY)
+        nc.scalar.copy(
+            out=x_bf[1][:].rearrange("p (c i) j -> p c j i", i=4),
+            in_=picked[:].rearrange("p j (c i) -> p c j i", i=4),
         )
-        prepare_w(nc.scalar.copy, 0, block(1), "01", "w_bf01", "w_codes01", "w_scales01")
-        quantize_x(1)
-        y[0, 0] = keep.tile([P, V], F32, name="y00")
-        for h in range(2):
-            cols = slice(h * P, (h + 1) * P)
-            acc = psum.tile([P, P], F32, name=f"acc_first{h}")
-            nc.tensor.matmul_mx(
-                out=acc[:],
-                lhsT=w_codes[0, 0].bitcast(FP8X4),
-                lhsT_scale=w_scales[0, 0],
-                rhs=x_codes[0][:, cols].bitcast(FP8X4),
-                rhs_scale=x_scales[0][:, cols],
-                start=True,
-                stop=True,
-            )
-            nc.scalar.copy(out=y[0, 0][:, cols], in_=acc[:])
-        scatter(0, 0)
-        prepare_w(nc.scalar.copy, 1, slice(0, N), "1", "first_codes", "w_codes1", "w_scales1")
-        product(0, 1, "w_raw1")
-        scatter(0, 1)
-        product(1, 0, "y10")
-        scatter(1, 0)
-        finish(0, nc.gpsimd, nc.scalar, (0, 320, U))
-        product(1, 1, "y11")
-        scatter(1, 1)
+        cast_w(nc.vector.tensor_copy, 0, 0)
+        quantize(x_codes[0], x_scales[0], x_bf[0])
+        quantize_w(0, 0)
+        product(0, 0)
+        cast_w(nc.vector.tensor_copy, 1, 0)
+        quantize(x_codes[1], x_scales[1], x_bf[1])
+        quantize_w(1, 0)
+        product(1, 0)
+        cast_w(nc.scalar.copy, 0, 1)
+        cast_w(nc.vector.tensor_copy, 1, 1)
+        quantize_w(0, 1)
+        product(0, 1)
+        quantize_w(1, 1)
+        product(1, 1)
+        y[0] = reused.tile([P, TAPS, V], F32, name="y0", offset=RAW_BYTES // 2)
+        y[1] = keep.tile([P, TAPS, V], F32, name="y1")
+        empty(nc.scalar.copy, 0, 0)
+        scatter_v(0, 0)
+        empty(nc.scalar.copy, 1, 0)
+        scatter_s(1, 0)
+        empty(nc.vector.tensor_copy, 0, 1)
+        empty(nc.scalar.copy, 1, 1)
+        scatter_v(0, 1)
+        scatter_s(1, 1)
+        finish(0, nc.gpsimd, nc.sync, (0, 320, U))
         finish(1, nc.vector, nc.sync, (0, 192, 384, U))

@@ -20,7 +20,6 @@ PACK = 4
 TAPS = 2
 BLOCKS = N // P
 LIST_COLS = V // 16
-RAW_BYTES = PACK * P * 4
 
 
 def tile_picked_spconv_none_e_kernel(tc, xT, w1, w2, offs, to1, to2, out):
@@ -28,16 +27,13 @@ def tile_picked_spconv_none_e_kernel(tc, xT, w1, w2, offs, to1, to2, out):
     with ExitStack() as ctx:
         lists = ctx.enter_context(tc.tile_pool(name="lists", bufs=1))
         keep = ctx.enter_context(tc.tile_pool(name="keep", bufs=1))
-        reused = ctx.enter_context(tc.tile_pool(name="reused", bufs=1))
         psum = ctx.enter_context(tc.psum_pool(name="psum", bufs=1))
 
         offs_sb = lists.tile([P, S // 16], U16, name="offs_sb")
         to_sb = [lists.tile([P, LIST_COLS], U16, name=f"to_sb{d}") for d in range(TAPS)]
         planes = [keep.tile([P, T], F32, name=f"plane{j}") for j in range(PACK)]
         x_rows = xT.rearrange("(p j) t -> p j t", j=PACK)
-        w_raw = {(d, 0): keep.tile([P, PACK, P], F32, name=f"w_raw{d}0") for d in range(TAPS)}
-        for d in range(TAPS):
-            w_raw[d, 1] = reused.tile([P, PACK, P], F32, name=f"w_raw{d}1", offset=d * RAW_BYTES)
+        w_raw = {(d, b): keep.tile([P, PACK, P], F32, name=f"w_raw{d}{b}", tag=f"w_raw{d}{b}", align_bytes=64) for d in range(TAPS) for b in range(BLOCKS)}
         w_rows = [w.rearrange("(p j) m -> p j m", j=PACK) for w in (w1, w2)]
 
         nc.sync.dma_start(out=planes[0][:], in_=x_rows[:, 0, :])
@@ -46,10 +42,9 @@ def tile_picked_spconv_none_e_kernel(tc, xT, w1, w2, offs, to1, to2, out):
             nc.sync.dma_start(out=planes[j][:], in_=x_rows[:, j, :])
         for d in range(TAPS):
             nc.sync.dma_start(out=w_raw[d, 0][:], in_=w_rows[d][:, :, 0:P])
-        nc.sync.dma_start(to_sb[0][:], to1)
-        nc.sync.dma_start(to_sb[1][:], to2)
-        for d in range(TAPS):
+        for d, to in enumerate((to1, to2)):
             nc.sync.dma_start(out=w_raw[d, 1][:], in_=w_rows[d][:, :, P:N])
+            nc.sync.dma_start(to_sb[d][:], to)
 
         windows = {}
         for d in range(TAPS):
@@ -61,9 +56,9 @@ def tile_picked_spconv_none_e_kernel(tc, xT, w1, w2, offs, to1, to2, out):
                     nc.scalar.activation(windows[d, b][:], windows[0, b][:], COPY)
 
         x_bf = [keep.tile([P, V, PACK], BF16, name=f"x_bf{d}", align_bytes=64) for d in range(TAPS)]
-        x_codes = [keep.tile([P, V], U32, name=f"x_codes{d}", align_bytes=64) for d in range(TAPS)]
+        x_codes = {0: keep.tile([P, V], U32, name="x_codes0", align_bytes=64)}
         x_scales = [keep.tile([P, V], U8, name=f"x_scales{d}", align_bytes=64) for d in range(TAPS)]
-        picked = keep.tile([P, PACK, V], BF16, name="picked")
+        picked = [keep.tile([P, 2, V], BF16, name=f"picked{h}") for h in range(2)]
 
         def tap_list(d):
             return offs_sb[:, d * LIST_COLS : (d + 1) * LIST_COLS]
@@ -77,7 +72,7 @@ def tile_picked_spconv_none_e_kernel(tc, xT, w1, w2, offs, to1, to2, out):
         w_bf, w_codes, w_scales = {}, {}, {}
 
         def cast_w(copy, d, b):
-            w_bf[d, b] = keep.tile([P, P, PACK], BF16, name=f"w_bf{d}{b}", align_bytes=64)
+            w_bf[d, b] = keep.tile([P, P, PACK], BF16, name=f"w_bf{d}{b}", tag=f"w_bf{d}{b}", align_bytes=64)
             copy(
                 out=w_bf[d, b][:].rearrange("p (c i) j -> p c j i", i=4),
                 in_=w_raw[d, b][:].rearrange("p j (c i) -> p c j i", i=4),
@@ -89,11 +84,14 @@ def tile_picked_spconv_none_e_kernel(tc, xT, w1, w2, offs, to1, to2, out):
             quantize(w_codes[d, b], w_scales[d, b], w_bf[d, b])
 
         acc, y = {}, {}
+        late_bank = psum.tile([P, TAPS, V], F32, name="late_bank")
+        for d in range(TAPS):
+            acc[d, 0] = psum.tile([P, V], F32, name=f"acc{d}0")[:]
+            acc[d, 1] = late_bank[:, d, :]
 
         def product(d, b):
-            acc[d, b] = psum.tile([P, V], F32, name=f"acc{d}{b}")
             nc.tensor.matmul_mx(
-                out=acc[d, b][:],
+                out=acc[d, b],
                 lhsT=w_codes[d, b][:].bitcast(FP8X4),
                 lhsT_scale=w_scales[d, b][:],
                 rhs=x_codes[d][:].bitcast(FP8X4),
@@ -102,14 +100,15 @@ def tile_picked_spconv_none_e_kernel(tc, xT, w1, w2, offs, to1, to2, out):
                 stop=True,
             )
 
-        def empty(copy, d, b):
-            copy(out=y[b][:, d, :], in_=acc[d, b][:])
+        def empty(copy, d, b, tag):
+            y[d, b] = keep.tile([P, V], F32, name=f"y{d}{b}", tag=tag, align_bytes=64)[:]
+            copy(out=y[d, b], in_=acc[d, b])
 
         def scatter_v(d, b):
-            nc.vector.tensor_copy(windows[d, b][:].indirect(to_sb[d][:]), y[b][:, d, :])
+            nc.vector.tensor_copy(windows[d, b][:].indirect(to_sb[d][:]), y[d, b])
 
         def scatter_s(d, b):
-            nc.scalar.activation(windows[d, b][:].indirect(to_sb[d][:]), y[b][:, d, :], COPY)
+            nc.scalar.activation(windows[d, b][:].indirect(to_sb[d][:]), y[d, b], COPY)
 
         def finish(b, engine, queue, edges):
             total = keep.tile([P, U], F32, name=f"total{b}")
@@ -120,34 +119,31 @@ def tile_picked_spconv_none_e_kernel(tc, xT, w1, w2, offs, to1, to2, out):
 
         for j in range(PACK):
             nc.vector.tensor_copy(x_bf[0][:, :, j], planes[j][:].indirect(tap_list(0)))
-            nc.scalar.activation(picked[:, j, :], planes[j][:].indirect(tap_list(1)), COPY)
-        nc.scalar.copy(
-            out=x_bf[1][:].rearrange("p (c i) j -> p c j i", i=4),
-            in_=picked[:].rearrange("p j (c i) -> p c j i", i=4),
-        )
-        cast_w(nc.vector.tensor_copy, 0, 0)
+            nc.scalar.activation(picked[j // 2][:, j % 2, :], planes[j][:].indirect(tap_list(1)), COPY)
+            if j % 2 == 1:
+                nc.vector.tensor_copy(out=x_bf[1][:, :, j - 1 : j + 1], in_=picked[j // 2][:].rearrange("p e v -> p v e"))
+        cast_w(nc.scalar.copy, 0, 0)
         quantize(x_codes[0], x_scales[0], x_bf[0])
         quantize_w(0, 0)
         product(0, 0)
-        cast_w(nc.vector.tensor_copy, 1, 0)
+        cast_w(nc.scalar.copy, 1, 0)
+        x_codes[1] = keep.tile([P, V], U32, name="x_codes1", tag="w_raw00", align_bytes=64)
         quantize(x_codes[1], x_scales[1], x_bf[1])
         quantize_w(1, 0)
         product(1, 0)
+        empty(nc.scalar.copy, 0, 0, "y00")
         cast_w(nc.scalar.copy, 0, 1)
         cast_w(nc.vector.tensor_copy, 1, 1)
+        scatter_s(0, 0)
         quantize_w(0, 1)
         product(0, 1)
+        empty(nc.vector.tensor_copy, 1, 0, "w_raw11")
         quantize_w(1, 1)
         product(1, 1)
-        y[0] = reused.tile([P, TAPS, V], F32, name="y0", offset=RAW_BYTES // 2)
-        y[1] = keep.tile([P, TAPS, V], F32, name="y1")
-        empty(nc.scalar.copy, 0, 0)
-        scatter_v(0, 0)
-        empty(nc.scalar.copy, 1, 0)
-        scatter_s(1, 0)
-        empty(nc.vector.tensor_copy, 0, 1)
-        empty(nc.scalar.copy, 1, 1)
-        scatter_v(0, 1)
-        scatter_s(1, 1)
+        scatter_v(1, 0)
+        empty(nc.scalar.copy, 0, 1, "y01")
+        empty(nc.scalar.copy, 1, 1, "y11")
+        scatter_s(0, 1)
+        scatter_v(1, 1)
         finish(0, nc.gpsimd, nc.sync, (0, 320, U))
         finish(1, nc.vector, nc.sync, (0, 192, 384, U))

@@ -42,8 +42,9 @@ def tile_picked_spconv_none_e_kernel(tc, xT, w1, w2, offs, to1, to2, out):
             nc.sync.dma_start(out=planes[j][:], in_=x_rows[:, j, :])
         for d in range(TAPS):
             nc.sync.dma_start(out=w_raw[d, 0][:], in_=w_rows[d][:, :, 0:P])
-        for d, to in enumerate((to1, to2)):
+        for d in range(TAPS):
             nc.sync.dma_start(out=w_raw[d, 1][:], in_=w_rows[d][:, :, P:N])
+        for d, to in enumerate((to1, to2)):
             nc.sync.dma_start(to_sb[d][:], to)
 
         windows = {}
@@ -146,4 +147,4 @@ def tile_picked_spconv_none_e_kernel(tc, xT, w1, w2, offs, to1, to2, out):
         scatter_s(0, 1)
         scatter_v(1, 1)
         finish(0, nc.gpsimd, nc.sync, (0, 320, U))
-        finish(1, nc.vector, nc.sync, (0, 192, 384, U))
+        finish(1, nc.vector, nc.scalar, (0, 192, 384, U))

@@ -147,4 +147,4 @@ def tile_picked_spconv_none_e_kernel(tc, xT, w1, w2, offs, to1, to2, out):
         scatter_s(0, 1)
         scatter_v(1, 1)
         finish(0, nc.gpsimd, nc.sync, (0, 320, U))
-        finish(1, nc.vector, nc.scalar, (0, 192, 384, U))
+        finish(1, nc.vector, nc.sync, (0, 192, 384, U))

@@ -142,8 +142,8 @@ def tile_picked_spconv_none_e_kernel(tc, xT, w1, w2, offs, to1, to2, out):
         quantize_w(1, 1)
         product(1, 1)
         scatter_v(1, 0)
-        empty(nc.scalar.copy, 0, 1, "y01")
         empty(nc.scalar.copy, 1, 1, "y11")
+        empty(nc.scalar.copy, 0, 1, "y01")
         scatter_s(0, 1)
         scatter_v(1, 1)
         finish(0, nc.gpsimd, nc.sync, (0, 320, U))

@@ -7,7 +7,6 @@ FLOPS = 2 * K * N * S
 
 F32 = mybir.dt.float32
 BF16 = mybir.dt.bfloat16
-I32 = mybir.dt.int32
 U32 = mybir.dt.uint32
 U16 = mybir.dt.uint16
 U8 = mybir.dt.uint8
@@ -19,7 +18,8 @@ P = 128
 PACK = 4
 TAPS = 2
 BLOCKS = N // P
-LIST_COLS = V // 16
+GROUP = 16
+EARLY = 192
 
 
 def tile_picked_spconv_none_e_kernel(tc, xT, w1, w2, offs, to1, to2, out):
@@ -29,122 +29,117 @@ def tile_picked_spconv_none_e_kernel(tc, xT, w1, w2, offs, to1, to2, out):
         keep = ctx.enter_context(tc.tile_pool(name="keep", bufs=1))
         psum = ctx.enter_context(tc.psum_pool(name="psum", bufs=1))
 
-        offs_sb = lists.tile([P, S // 16], U16, name="offs_sb")
-        to_sb = [lists.tile([P, LIST_COLS], U16, name=f"to_sb{d}") for d in range(TAPS)]
+        picks = lists.tile([P, S // GROUP], U16, name="picks")
+        places = [lists.tile([P, V // GROUP], U16, name=f"places{d}") for d in range(TAPS)]
         planes = [keep.tile([P, T], F32, name=f"plane{j}") for j in range(PACK)]
+        raw = {(d, b): keep.tile([P, PACK, P], F32, name=f"raw{d}{b}", tag=f"raw{d}{b}", align_bytes=64) for d in range(TAPS) for b in range(BLOCKS)}
         x_rows = xT.rearrange("(p j) t -> p j t", j=PACK)
-        w_raw = {(d, b): keep.tile([P, PACK, P], F32, name=f"w_raw{d}{b}", tag=f"w_raw{d}{b}", align_bytes=64) for d in range(TAPS) for b in range(BLOCKS)}
         w_rows = [w.rearrange("(p j) m -> p j m", j=PACK) for w in (w1, w2)]
 
-        nc.sync.dma_start(out=planes[0][:], in_=x_rows[:, 0, :])
-        nc.sync.dma_start(offs_sb[:], offs)
-        for j in range(1, PACK):
-            nc.sync.dma_start(out=planes[j][:], in_=x_rows[:, j, :])
-        for d in range(TAPS):
-            nc.sync.dma_start(out=w_raw[d, 0][:], in_=w_rows[d][:, :, 0:P])
-        for d in range(TAPS):
-            nc.sync.dma_start(out=w_raw[d, 1][:], in_=w_rows[d][:, :, P:N])
-        for d, to in enumerate((to1, to2)):
-            nc.sync.dma_start(to_sb[d][:], to)
-
-        windows = {}
-        for d in range(TAPS):
-            for b in range(BLOCKS):
-                windows[d, b] = keep.tile([P, U], F32, name=f"window{d}{b}")
-                if d == 0:
-                    nc.vector.memset(windows[d, b][:], 0.0)
-                else:
-                    nc.scalar.activation(windows[d, b][:], windows[0, b][:], COPY)
-
-        x_bf = [keep.tile([P, V, PACK], BF16, name=f"x_bf{d}", align_bytes=64) for d in range(TAPS)]
-        x_codes = {0: keep.tile([P, V], U32, name="x_codes0", align_bytes=64)}
-        x_scales = [keep.tile([P, V], U8, name=f"x_scales{d}", align_bytes=64) for d in range(TAPS)]
-        picked = [keep.tile([P, 2, V], BF16, name=f"picked{h}") for h in range(2)]
-
-        def tap_list(d):
-            return offs_sb[:, d * LIST_COLS : (d + 1) * LIST_COLS]
-
-        def block(b):
+        def rows(b):
             return slice(b * P, (b + 1) * P)
 
-        def quantize(codes, scales, src):
+        def entries(tile, first, last):
+            return tile[:, first // GROUP : last // GROUP]
+
+        nc.sync.dma_start(out=planes[0][:], in_=x_rows[:, 0, :])
+        nc.sync.dma_start(picks[:], offs)
+        for j in range(1, PACK):
+            nc.sync.dma_start(out=planes[j][:], in_=x_rows[:, j, :])
+        for b in range(BLOCKS):
+            for d in range(TAPS):
+                nc.sync.dma_start(out=raw[d, b][:], in_=w_rows[d][:, :, rows(b)])
+        for d, to in enumerate((to1, to2)):
+            nc.sync.dma_start(places[d][:], to)
+
+        target = {}
+        for d in range(TAPS):
+            for b in range(BLOCKS):
+                target[d, b] = keep.tile([P, U], F32, name=f"target{d}{b}")
+                if d == 0:
+                    nc.vector.memset(target[d, b][:], 0.0)
+                else:
+                    nc.scalar.activation(target[d, b][:], target[0, b][:], COPY)
+
+        x_bf = [keep.tile([P, V, PACK], BF16, name=f"x_bf{d}", align_bytes=64) for d in range(TAPS)]
+        picked = [keep.tile([P, 2, V], BF16, name=f"picked{h}") for h in range(2)]
+        for j in range(PACK):
+            nc.vector.tensor_copy(x_bf[0][:, :, j], planes[j][:].indirect(entries(picks, 0, V)))
+            nc.scalar.activation(picked[j // 2][:, j % 2, :], planes[j][:].indirect(entries(picks, V, S)), COPY)
+            if j % 2 == 1:
+                nc.vector.tensor_copy(out=x_bf[1][:, :, j - 1 : j + 1], in_=picked[j // 2][:].rearrange("p e v -> p v e"))
+
+        def quantize(name, src, width, tag):
+            codes = keep.tile([P, width], U32, name=f"{name}_codes", tag=tag, align_bytes=64)
+            scales = keep.tile([P, width], U8, name=f"{name}_scales", align_bytes=64)
             nc.vector.quantize_mx(out=codes[:].bitcast(FP8X4), scales=scales[:], in_=src[:].rearrange("p v j -> p (v j)"))
+            return codes, scales
 
-        w_bf, w_codes, w_scales = {}, {}, {}
+        w_bf = {(d, b): keep.tile([P, P, PACK], BF16, name=f"w_bf{d}{b}", align_bytes=64) for d in range(TAPS) for b in range(BLOCKS)}
 
-        def cast_w(copy, d, b):
-            w_bf[d, b] = keep.tile([P, P, PACK], BF16, name=f"w_bf{d}{b}", tag=f"w_bf{d}{b}", align_bytes=64)
-            copy(
-                out=w_bf[d, b][:].rearrange("p (c i) j -> p c j i", i=4),
-                in_=w_raw[d, b][:].rearrange("p j (c i) -> p c j i", i=4),
+        def round_w(d, b, first, last):
+            nc.scalar.copy(
+                out=w_bf[d, b][:, first:last, :].rearrange("p (c i) j -> p c j i", i=4),
+                in_=raw[d, b][:, :, first:last].rearrange("p j (c i) -> p c j i", i=4),
             )
 
-        def quantize_w(d, b):
-            w_codes[d, b] = keep.tile([P, P], U32, name=f"w_codes{d}{b}", align_bytes=64)
-            w_scales[d, b] = keep.tile([P, P], U8, name=f"w_scales{d}{b}", align_bytes=64)
-            quantize(w_codes[d, b], w_scales[d, b], w_bf[d, b])
-
-        acc, y = {}, {}
-        late_bank = psum.tile([P, TAPS, V], F32, name="late_bank")
-        for d in range(TAPS):
-            acc[d, 0] = psum.tile([P, V], F32, name=f"acc{d}0")[:]
-            acc[d, 1] = late_bank[:, d, :]
+        tap0_bank = psum.tile([P, BLOCKS * V], F32, name="tap0_bank")
+        acc = {(0, b): tap0_bank[:, b * V : (b + 1) * V] for b in range(BLOCKS)}
+        for b in range(BLOCKS):
+            acc[1, b] = psum.tile([P, V], F32, name=f"acc1{b}")[:]
+        x_mx = {}
 
         def product(d, b):
+            w_codes, w_scales = quantize(f"w{d}{b}", w_bf[d, b], P, f"w{d}{b}_codes")
+            x_codes, x_scales = x_mx[d]
             nc.tensor.matmul_mx(
                 out=acc[d, b],
-                lhsT=w_codes[d, b][:].bitcast(FP8X4),
-                lhsT_scale=w_scales[d, b][:],
-                rhs=x_codes[d][:].bitcast(FP8X4),
-                rhs_scale=x_scales[d][:],
+                lhsT=w_codes[:].bitcast(FP8X4),
+                lhsT_scale=w_scales[:],
+                rhs=x_codes[:].bitcast(FP8X4),
+                rhs_scale=x_scales[:],
                 start=True,
                 stop=True,
             )
 
-        def empty(copy, d, b, tag):
-            y[d, b] = keep.tile([P, V], F32, name=f"y{d}{b}", tag=tag, align_bytes=64)[:]
-            copy(out=y[d, b], in_=acc[d, b])
+        y0 = keep.tile([P, BLOCKS * V], F32, name="y0", tag="raw10", align_bytes=64)
+        y1 = {}
 
-        def scatter_v(d, b):
-            nc.vector.tensor_copy(windows[d, b][:].indirect(to_sb[d][:]), y[d, b])
+        def empty1(copy, b, tag):
+            y1[b] = keep.tile([P, V], F32, name=f"y1{b}", tag=tag, align_bytes=64)
+            copy(out=y1[b][:], in_=acc[1, b])
 
-        def scatter_s(d, b):
-            nc.scalar.activation(windows[d, b][:].indirect(to_sb[d][:]), y[d, b], COPY)
+        def scatter0(b, first, last):
+            nc.scalar.activation(target[0, b][:].indirect(entries(places[0], first, last)), y0[:, b * V + first : b * V + last], COPY)
 
-        def finish(b, engine, queue, edges):
+        def scatter1(b):
+            nc.vector.tensor_copy(target[1, b][:].indirect(places[1][:]), y1[b][:])
+
+        def finish(b, engine, edges):
             total = keep.tile([P, U], F32, name=f"total{b}")
             for h in range(len(edges) - 1):
                 cols = slice(edges[h], edges[h + 1])
-                engine.tensor_tensor(total[:, cols], windows[0, b][:, cols], windows[1, b][:, cols], ADD)
-                queue.dma_start(out=out[block(b), cols], in_=total[:, cols])
+                engine.tensor_tensor(total[:, cols], target[0, b][:, cols], target[1, b][:, cols], ADD)
+                nc.sync.dma_start(out=out[rows(b), cols], in_=total[:, cols])
 
-        for j in range(PACK):
-            nc.vector.tensor_copy(x_bf[0][:, :, j], planes[j][:].indirect(tap_list(0)))
-            nc.scalar.activation(picked[j // 2][:, j % 2, :], planes[j][:].indirect(tap_list(1)), COPY)
-            if j % 2 == 1:
-                nc.vector.tensor_copy(out=x_bf[1][:, :, j - 1 : j + 1], in_=picked[j // 2][:].rearrange("p e v -> p v e"))
-        cast_w(nc.scalar.copy, 0, 0)
-        quantize(x_codes[0], x_scales[0], x_bf[0])
-        quantize_w(0, 0)
+        round_w(0, 0, 0, P)
+        x_mx[0] = quantize("x0", x_bf[0], V, "x0_codes")
         product(0, 0)
-        cast_w(nc.scalar.copy, 1, 0)
-        x_codes[1] = keep.tile([P, V], U32, name="x_codes1", tag="w_raw00", align_bytes=64)
-        quantize(x_codes[1], x_scales[1], x_bf[1])
-        quantize_w(1, 0)
+        round_w(1, 0, 0, P)
+        x_mx[1] = quantize("x1", x_bf[1], V, "raw00")
         product(1, 0)
-        empty(nc.scalar.copy, 0, 0, "y00")
-        cast_w(nc.scalar.copy, 0, 1)
-        cast_w(nc.vector.tensor_copy, 1, 1)
-        scatter_s(0, 0)
-        quantize_w(0, 1)
+        round_w(0, 1, 0, P)
+        round_w(1, 1, 0, P)
+        nc.vector.tensor_copy(out=y0[:, :EARLY], in_=tap0_bank[:, :EARLY])
+        scatter0(0, 0, EARLY)
         product(0, 1)
-        empty(nc.vector.tensor_copy, 1, 0, "w_raw11")
-        quantize_w(1, 1)
+        empty1(nc.vector.tensor_copy, 0, "raw01")
         product(1, 1)
-        scatter_v(1, 0)
-        empty(nc.scalar.copy, 1, 1, "y11")
-        empty(nc.scalar.copy, 0, 1, "y01")
-        scatter_s(0, 1)
-        scatter_v(1, 1)
-        finish(0, nc.gpsimd, nc.sync, (0, 320, U))
-        finish(1, nc.vector, nc.sync, (0, 192, 384, U))
+        scatter1(0)
+        nc.scalar.copy(out=y0[:, EARLY:], in_=tap0_bank[:, EARLY:])
+        empty1(nc.scalar.copy, 1, "y11")
+        scatter0(0, EARLY, V)
+        scatter0(1, 0, V)
+        scatter1(1)
+        finish(0, nc.gpsimd, (0, 320, U))
+        finish(1, nc.vector, (0, 192, 384, U))

@@ -85,22 +85,24 @@ def tile_picked_spconv_none_e_kernel(tc, xT, w1, w2, offs, to1, to2, out):
 
         tap0_bank = psum.tile([P, BLOCKS * V], F32, name="tap0_bank")
         acc = {(0, b): tap0_bank[:, b * V : (b + 1) * V] for b in range(BLOCKS)}
-        for b in range(BLOCKS):
-            acc[1, b] = psum.tile([P, V], F32, name=f"acc1{b}")[:]
+        acc[1, 1] = psum.tile([P, V], F32, name="acc11")[:]
+        half_banks = [psum.tile([P, P], F32, name=f"acc10_{h}") for h in range(2)]
         x_mx = {}
 
         def product(d, b):
             w_codes, w_scales = quantize(f"w{d}{b}", w_bf[d, b], P, f"w{d}{b}_codes")
             x_codes, x_scales = x_mx[d]
-            nc.tensor.matmul_mx(
-                out=acc[d, b],
-                lhsT=w_codes[:].bitcast(FP8X4),
-                lhsT_scale=w_scales[:],
-                rhs=x_codes[:].bitcast(FP8X4),
-                rhs_scale=x_scales[:],
-                start=True,
-                stop=True,
-            )
+            parts = [(acc[d, b], slice(0, V))] if (d, b) in acc else [(half_banks[h][:], rows(h)) for h in range(2)]
+            for bank, cols in parts:
+                nc.tensor.matmul_mx(
+                    out=bank,
+                    lhsT=w_codes[:].bitcast(FP8X4),
+                    lhsT_scale=w_scales[:],
+                    rhs=x_codes[:, cols].bitcast(FP8X4),
+                    rhs_scale=x_scales[:, cols],
+                    start=True,
+                    stop=True,
+                )
 
         y0 = keep.tile([P, BLOCKS * V], F32, name="y0", tag="raw10", align_bytes=64)
         y1 = {}
@@ -133,7 +135,9 @@ def tile_picked_spconv_none_e_kernel(tc, xT, w1, w2, offs, to1, to2, out):
         nc.vector.tensor_copy(out=y0[:, :EARLY], in_=tap0_bank[:, :EARLY])
         scatter0(0, 0, EARLY)
         product(0, 1)
-        empty1(nc.vector.tensor_copy, 0, "raw01")
+        y1[0] = keep.tile([P, V], F32, name="y10", tag="raw01", align_bytes=64)
+        for h in range(2):
+            nc.vector.tensor_copy(out=y1[0][:, rows(h)], in_=half_banks[h][:])
         product(1, 1)
         scatter1(0)
         nc.scalar.copy(out=y0[:, EARLY:], in_=tap0_bank[:, EARLY:])

@@ -20,6 +20,7 @@ TAPS = 2
 BLOCKS = N // P
 GROUP = 16
 EARLY = 192
+SHARE = 64
 
 
 def tile_picked_spconv_none_e_kernel(tc, xT, w1, w2, offs, to1, to2, out):
@@ -66,19 +67,24 @@ def tile_picked_spconv_none_e_kernel(tc, xT, w1, w2, offs, to1, to2, out):
         for j in range(PACK):
             nc.vector.tensor_copy(x_bf[0][:, :, j], planes[j][:].indirect(entries(picks, 0, V)))
             nc.scalar.activation(picked[j // 2][:, j % 2, :], planes[j][:].indirect(entries(picks, V, S)), COPY)
-            if j % 2 == 1:
-                nc.vector.tensor_copy(out=x_bf[1][:, :, j - 1 : j + 1], in_=picked[j // 2][:].rearrange("p e v -> p v e"))
+            if j == 1:
+                nc.scalar.copy(out=x_bf[1][:, :P, 0:2], in_=picked[0][:, :, :P].rearrange("p e v -> p v e"))
+                nc.vector.tensor_copy(out=x_bf[1][:, P:, 0:2], in_=picked[0][:, :, P:].rearrange("p e v -> p v e"))
+            if j == 3:
+                nc.vector.tensor_copy(out=x_bf[1][:, :, 2:4], in_=picked[1][:].rearrange("p e v -> p v e"))
 
-        def quantize(name, src, width, tag):
-            codes = keep.tile([P, width], U32, name=f"{name}_codes", tag=tag, align_bytes=64)
+        def quantize(name, src, width, codes):
             scales = keep.tile([P, width], U8, name=f"{name}_scales", align_bytes=64)
-            nc.vector.quantize_mx(out=codes[:].bitcast(FP8X4), scales=scales[:], in_=src[:].rearrange("p v j -> p (v j)"))
+            nc.vector.quantize_mx(out=codes.bitcast(FP8X4), scales=scales[:], in_=src.rearrange("p v j -> p (v j)"))
             return codes, scales
+
+        def words(name, width, tag):
+            return keep.tile([P, width], U32, name=name, tag=tag, align_bytes=64)
 
         w_bf = {(d, b): keep.tile([P, P, PACK], BF16, name=f"w_bf{d}{b}", align_bytes=64) for d in range(TAPS) for b in range(BLOCKS)}
 
-        def round_w(d, b, first, last):
-            nc.scalar.copy(
+        def round_w(d, b, first, last, copy=nc.scalar.copy):
+            copy(
                 out=w_bf[d, b][:, first:last, :].rearrange("p (c i) j -> p c j i", i=4),
                 in_=raw[d, b][:, :, first:last].rearrange("p j (c i) -> p c j i", i=4),
             )
@@ -89,22 +95,33 @@ def tile_picked_spconv_none_e_kernel(tc, xT, w1, w2, offs, to1, to2, out):
         half_banks = [psum.tile([P, P], F32, name=f"acc10_{h}") for h in range(2)]
         x_mx = {}
 
-        def product(d, b):
-            w_codes, w_scales = quantize(f"w{d}{b}", w_bf[d, b], P, f"w{d}{b}_codes")
-            x_codes, x_scales = x_mx[d]
-            parts = [(acc[d, b], slice(0, V))] if (d, b) in acc else [(half_banks[h][:], rows(h)) for h in range(2)]
-            for bank, cols in parts:
-                nc.tensor.matmul_mx(
-                    out=bank,
-                    lhsT=w_codes[:].bitcast(FP8X4),
-                    lhsT_scale=w_scales[:],
-                    rhs=x_codes[:, cols].bitcast(FP8X4),
-                    rhs_scale=x_scales[:, cols],
-                    start=True,
-                    stop=True,
-                )
+        w_mx = {}
 
-        y0 = keep.tile([P, BLOCKS * V], F32, name="y0", tag="raw10", align_bytes=64)
+        def quantize_w(d, b):
+            w_mx[d, b] = quantize(f"w{d}{b}", w_bf[d, b][:], P, words(f"w{d}{b}_codes", P, f"w{d}{b}_codes")[:])
+
+        def multiply(bank, d, b, part):
+            w_codes, w_scales = w_mx[d, b]
+            x_codes, x_scales = x_mx[part]
+            nc.tensor.matmul_mx(
+                out=bank,
+                lhsT=w_codes.bitcast(FP8X4),
+                lhsT_scale=w_scales[:],
+                rhs=x_codes.bitcast(FP8X4),
+                rhs_scale=x_scales[:],
+                start=True,
+                stop=True,
+            )
+
+        def product(d, b):
+            quantize_w(d, b)
+            if d == 0:
+                multiply(acc[d, b], d, b, 0)
+            else:
+                for h in range(2):
+                    multiply(acc[d, b][:, rows(h)], d, b, (1, h))
+
+        y0 = keep.tile([P, BLOCKS * V], F32, name="y0")
         y1 = {}
 
         def empty1(copy, b, tag):
@@ -125,14 +142,20 @@ def tile_picked_spconv_none_e_kernel(tc, xT, w1, w2, offs, to1, to2, out):
                 nc.sync.dma_start(out=out[rows(b), cols], in_=total[:, cols])
 
         round_w(0, 0, 0, P)
-        x_mx[0] = quantize("x0", x_bf[0], V, "x0_codes")
-        product(0, 0)
+        quantize_w(0, 0)
+        first_codes = words("first_codes", V + P, "raw00")
+        x_mx[0] = quantize("x0", x_bf[0][:], V, first_codes[:, :V])
+        multiply(acc[0, 0], 0, 0, 0)
         round_w(1, 0, 0, P)
-        x_mx[1] = quantize("x1", x_bf[1], V, "raw00")
-        product(1, 0)
+        x_mx[1, 0] = quantize("x10", x_bf[1][:, rows(0), :], P, first_codes[:, V:])
+        quantize_w(1, 0)
+        multiply(half_banks[0][:], 1, 0, (1, 0))
+        x_mx[1, 1] = quantize("x11", x_bf[1][:, rows(1), :], P, words("second_codes", P, "raw10")[:])
+        multiply(half_banks[1][:], 1, 0, (1, 1))
         round_w(0, 1, 0, P)
-        round_w(1, 1, 0, P)
-        nc.vector.tensor_copy(out=y0[:, :EARLY], in_=tap0_bank[:, :EARLY])
+        nc.scalar.copy(out=y0[:, :EARLY], in_=tap0_bank[:, :EARLY])
+        round_w(1, 1, 0, SHARE)
+        round_w(1, 1, SHARE, P, nc.vector.tensor_copy)
         scatter0(0, 0, EARLY)
         product(0, 1)
         y1[0] = keep.tile([P, V], F32, name="y10", tag="raw01", align_bytes=64)

@@ -20,7 +20,9 @@ TAPS = 2
 BLOCKS = N // P
 GROUP = 16
 EARLY = 192
-SHARE = 64
+SHARE = 56
+THIRD = 80
+RAW_BYTES = PACK * P * 4
 
 
 def tile_picked_spconv_none_e_kernel(tc, xT, w1, w2, offs, to1, to2, out):
@@ -28,12 +30,15 @@ def tile_picked_spconv_none_e_kernel(tc, xT, w1, w2, offs, to1, to2, out):
     with ExitStack() as ctx:
         lists = ctx.enter_context(tc.tile_pool(name="lists", bufs=1))
         keep = ctx.enter_context(tc.tile_pool(name="keep", bufs=1))
+        reused = ctx.enter_context(tc.tile_pool(name="reused", bufs=1))
         psum = ctx.enter_context(tc.psum_pool(name="psum", bufs=1))
 
         picks = lists.tile([P, S // GROUP], U16, name="picks")
         places = [lists.tile([P, V // GROUP], U16, name=f"places{d}") for d in range(TAPS)]
         planes = [keep.tile([P, T], F32, name=f"plane{j}") for j in range(PACK)]
-        raw = {(d, b): keep.tile([P, PACK, P], F32, name=f"raw{d}{b}", tag=f"raw{d}{b}", align_bytes=64) for d in range(TAPS) for b in range(BLOCKS)}
+        raw = {(d, d): keep.tile([P, PACK, P], F32, name=f"raw{d}{d}", tag=f"raw{d}{d}", align_bytes=64) for d in range(TAPS)}
+        raw[1, 0] = reused.tile([P, PACK, P], F32, name="raw10", offset=0, align_bytes=64)
+        raw[0, 1] = reused.tile([P, PACK, P], F32, name="raw01", offset=RAW_BYTES, align_bytes=64)
         x_rows = xT.rearrange("(p j) t -> p j t", j=PACK)
         w_rows = [w.rearrange("(p j) m -> p j m", j=PACK) for w in (w1, w2)]
 
@@ -81,7 +86,7 @@ def tile_picked_spconv_none_e_kernel(tc, xT, w1, w2, offs, to1, to2, out):
         def words(name, width, tag):
             return keep.tile([P, width], U32, name=name, tag=tag, align_bytes=64)
 
-        w_bf = {(d, b): keep.tile([P, P, PACK], BF16, name=f"w_bf{d}{b}", align_bytes=64) for d in range(TAPS) for b in range(BLOCKS)}
+        w_bf = {(d, 0): keep.tile([P, P, PACK], BF16, name=f"w_bf{d}0", align_bytes=64) for d in range(TAPS)}
 
         def round_w(d, b, first, last, copy=nc.scalar.copy):
             copy(
@@ -150,15 +155,20 @@ def tile_picked_spconv_none_e_kernel(tc, xT, w1, w2, offs, to1, to2, out):
         x_mx[1, 0] = quantize("x10", x_bf[1][:, rows(0), :], P, first_codes[:, V:])
         quantize_w(1, 0)
         multiply(half_banks[0][:], 1, 0, (1, 0))
-        x_mx[1, 1] = quantize("x11", x_bf[1][:, rows(1), :], P, words("second_codes", P, "raw10")[:])
+        w_bf[0, 1] = reused.tile([P, P, PACK], BF16, name="w_bf01", offset=RAW_BYTES // 2, align_bytes=64)
+        round_w(0, 1, THIRD, P, nc.vector.tensor_copy)
+        second_codes = reused.tile([P, P], U32, name="second_codes", offset=0, align_bytes=64)
+        x_mx[1, 1] = quantize("x11", x_bf[1][:, rows(1), :], P, second_codes[:])
         multiply(half_banks[1][:], 1, 0, (1, 1))
-        round_w(0, 1, 0, P)
+        round_w(0, 1, 0, THIRD)
+        quantize_w(0, 1)
+        w_bf[1, 1] = reused.tile([P, P, PACK], BF16, name="w_bf11", offset=RAW_BYTES + RAW_BYTES // 2, align_bytes=64)
         nc.scalar.copy(out=y0[:, :EARLY], in_=tap0_bank[:, :EARLY])
         round_w(1, 1, 0, SHARE)
         round_w(1, 1, SHARE, P, nc.vector.tensor_copy)
         scatter0(0, 0, EARLY)
-        product(0, 1)
-        y1[0] = keep.tile([P, V], F32, name="y10", tag="raw01", align_bytes=64)
+        multiply(acc[0, 1], 0, 1, 0)
+        y1[0] = reused.tile([P, V], F32, name="y10", offset=RAW_BYTES, align_bytes=64)
         for h in range(2):
             nc.vector.tensor_copy(out=y1[0][:, rows(h)], in_=half_banks[h][:])
         product(1, 1)

from contextlib import ExitStack

import concourse.mybir as mybir

K, T, S, V, N, U = 512, 1024, 512, 256, 256, 512
FLOPS = 2 * K * N * S

F32 = mybir.dt.float32
BF16 = mybir.dt.bfloat16
U32 = mybir.dt.uint32
U16 = mybir.dt.uint16
U8 = mybir.dt.uint8
FP8X4 = mybir.dt.float8_e4m3fn_x4
ADD = mybir.AluOpType.add
COPY = mybir.ActivationFunctionType.Copy

P = 128
PACK = 4
TAPS = 2
BLOCKS = N // P
GROUP = 16
EARLY = 192
SHARE = 56
THIRD = 80
RAW_BYTES = PACK * P * 4


def tile_picked_spconv_none_e_kernel(tc, xT, w1, w2, offs, to1, to2, out):
    nc = tc.nc
    with ExitStack() as ctx:
        lists = ctx.enter_context(tc.tile_pool(name="lists", bufs=1))
        keep = ctx.enter_context(tc.tile_pool(name="keep", bufs=1))
        reused = ctx.enter_context(tc.tile_pool(name="reused", bufs=1))
        psum = ctx.enter_context(tc.psum_pool(name="psum", bufs=1))

        picks = lists.tile([P, S // GROUP], U16, name="picks")
        places = [lists.tile([P, V // GROUP], U16, name=f"places{d}") for d in range(TAPS)]
        planes = [keep.tile([P, T], F32, name=f"plane{j}") for j in range(PACK)]
        raw = {(d, d): keep.tile([P, PACK, P], F32, name=f"raw{d}{d}", tag=f"raw{d}{d}", align_bytes=64) for d in range(TAPS)}
        raw[1, 0] = reused.tile([P, PACK, P], F32, name="raw10", offset=0, align_bytes=64)
        raw[0, 1] = reused.tile([P, PACK, P], F32, name="raw01", offset=RAW_BYTES, align_bytes=64)
        x_rows = xT.rearrange("(p j) t -> p j t", j=PACK)
        w_rows = [w.rearrange("(p j) m -> p j m", j=PACK) for w in (w1, w2)]

        def rows(b):
            return slice(b * P, (b + 1) * P)

        def entries(tile, first, last):
            return tile[:, first // GROUP : last // GROUP]

        nc.sync.dma_start(out=planes[0][:], in_=x_rows[:, 0, :])
        nc.sync.dma_start(picks[:], offs)
        for j in range(1, PACK):
            nc.sync.dma_start(out=planes[j][:], in_=x_rows[:, j, :])
        for b in range(BLOCKS):
            for d in range(TAPS):
                nc.sync.dma_start(out=raw[d, b][:], in_=w_rows[d][:, :, rows(b)])
        for d, to in enumerate((to1, to2)):
            nc.sync.dma_start(places[d][:], to)

        target = {}
        for d in range(TAPS):
            for b in range(BLOCKS):
                target[d, b] = keep.tile([P, U], F32, name=f"target{d}{b}")
                if d == 0:
                    nc.vector.memset(target[d, b][:], 0.0)
                else:
                    nc.scalar.activation(target[d, b][:], target[0, b][:], COPY)

        x_bf = [keep.tile([P, V, PACK], BF16, name=f"x_bf{d}", align_bytes=64) for d in range(TAPS)]
        picked = [keep.tile([P, 2, V], BF16, name=f"picked{h}") for h in range(2)]
        for j in range(PACK):
            nc.vector.tensor_copy(x_bf[0][:, :, j], planes[j][:].indirect(entries(picks, 0, V)))
            nc.scalar.activation(picked[j // 2][:, j % 2, :], planes[j][:].indirect(entries(picks, V, S)), COPY)
            if j == 1:
                nc.scalar.copy(out=x_bf[1][:, :P, 0:2], in_=picked[0][:, :, :P].rearrange("p e v -> p v e"))
                nc.vector.tensor_copy(out=x_bf[1][:, P:, 0:2], in_=picked[0][:, :, P:].rearrange("p e v -> p v e"))
            if j == 3:
                nc.vector.tensor_copy(out=x_bf[1][:, :, 2:4], in_=picked[1][:].rearrange("p e v -> p v e"))

        def quantize(name, src, width, codes):
            scales = keep.tile([P, width], U8, name=f"{name}_scales", align_bytes=64)
            nc.vector.quantize_mx(out=codes.bitcast(FP8X4), scales=scales[:], in_=src.rearrange("p v j -> p (v j)"))
            return codes, scales

        def words(name, width, tag):
            return keep.tile([P, width], U32, name=name, tag=tag, align_bytes=64)

        w_bf = {(d, 0): keep.tile([P, P, PACK], BF16, name=f"w_bf{d}0", align_bytes=64) for d in range(TAPS)}

        def round_w(d, b, first, last, copy=nc.scalar.copy):
            copy(
                out=w_bf[d, b][:, first:last, :].rearrange("p (c i) j -> p c j i", i=4),
                in_=raw[d, b][:, :, first:last].rearrange("p j (c i) -> p c j i", i=4),
            )

        tap0_bank = psum.tile([P, BLOCKS * V], F32, name="tap0_bank")
        acc = {(0, b): tap0_bank[:, b * V : (b + 1) * V] for b in range(BLOCKS)}
        acc[1, 1] = psum.tile([P, V], F32, name="acc11")[:]
        half_banks = [psum.tile([P, P], F32, name=f"acc10_{h}") for h in range(2)]
        x_mx = {}

        w_mx = {}

        def quantize_w(d, b):
            w_mx[d, b] = quantize(f"w{d}{b}", w_bf[d, b][:], P, words(f"w{d}{b}_codes", P, f"w{d}{b}_codes")[:])

        def multiply(bank, d, b, part):
            w_codes, w_scales = w_mx[d, b]
            x_codes, x_scales = x_mx[part]
            nc.tensor.matmul_mx(
                out=bank,
                lhsT=w_codes.bitcast(FP8X4),
                lhsT_scale=w_scales[:],
                rhs=x_codes.bitcast(FP8X4),
                rhs_scale=x_scales[:],
                start=True,
                stop=True,
            )

        def product(d, b):
            quantize_w(d, b)
            if d == 0:
                multiply(acc[d, b], d, b, 0)
            else:
                for h in range(2):
                    multiply(acc[d, b][:, rows(h)], d, b, (1, h))

        y0 = keep.tile([P, BLOCKS * V], F32, name="y0")
        y1 = {}

        def empty1(copy, b, tag):
            y1[b] = keep.tile([P, V], F32, name=f"y1{b}", tag=tag, align_bytes=64)
            copy(out=y1[b][:], in_=acc[1, b])

        def scatter0(b, first, last):
            nc.scalar.activation(target[0, b][:].indirect(entries(places[0], first, last)), y0[:, b * V + first : b * V + last], COPY)

        def scatter1(b):
            nc.vector.tensor_copy(target[1, b][:].indirect(places[1][:]), y1[b][:])

        def finish(b, engine, edges):
            total = keep.tile([P, U], F32, name=f"total{b}")
            for h in range(len(edges) - 1):
                cols = slice(edges[h], edges[h + 1])
                engine.tensor_tensor(total[:, cols], target[0, b][:, cols], target[1, b][:, cols], ADD)
                nc.sync.dma_start(out=out[rows(b), cols], in_=total[:, cols])

        round_w(0, 0, 0, P)
        quantize_w(0, 0)
        first_codes = words("first_codes", V + P, "raw00")
        x_mx[0] = quantize("x0", x_bf[0][:], V, first_codes[:, :V])
        multiply(acc[0, 0], 0, 0, 0)
        round_w(1, 0, 0, P)
        x_mx[1, 0] = quantize("x10", x_bf[1][:, rows(0), :], P, first_codes[:, V:])
        quantize_w(1, 0)
        multiply(half_banks[0][:], 1, 0, (1, 0))
        w_bf[0, 1] = reused.tile([P, P, PACK], BF16, name="w_bf01", offset=RAW_BYTES // 2, align_bytes=64)
        round_w(0, 1, THIRD, P, nc.vector.tensor_copy)
        second_codes = reused.tile([P, P], U32, name="second_codes", offset=0, align_bytes=64)
        x_mx[1, 1] = quantize("x11", x_bf[1][:, rows(1), :], P, second_codes[:])
        multiply(half_banks[1][:], 1, 0, (1, 1))
        round_w(0, 1, 0, THIRD)
        quantize_w(0, 1)
        w_bf[1, 1] = reused.tile([P, P, PACK], BF16, name="w_bf11", offset=RAW_BYTES + RAW_BYTES // 2, align_bytes=64)
        nc.scalar.copy(out=y0[:, :EARLY], in_=tap0_bank[:, :EARLY])
        round_w(1, 1, 0, SHARE)
        round_w(1, 1, SHARE, P, nc.vector.tensor_copy)
        scatter0(0, 0, EARLY)
        multiply(acc[0, 1], 0, 1, 0)
        y1[0] = reused.tile([P, V], F32, name="y10", offset=RAW_BYTES, align_bytes=64)
        for h in range(2):
            nc.vector.tensor_copy(out=y1[0][:, rows(h)], in_=half_banks[h][:])
        product(1, 1)
        scatter1(0)
        nc.scalar.copy(out=y0[:, EARLY:], in_=tap0_bank[:, EARLY:])
        empty1(nc.scalar.copy, 1, "y11")
        scatter0(0, EARLY, V)
        scatter0(1, 0, V)
        scatter1(1)
        finish(0, nc.gpsimd, (0, 320, U))
        finish(1, nc.vector, (0, 192, 384, U))
